import numpy as np
import ml_dtypes


def mxq(x, axis, fmt="e4m3"):
    dtype, down = {"e4m3": (ml_dtypes.float8_e4m3fn, 7), "e5m2": (ml_dtypes.float8_e5m2, 14)}[fmt]
    v = np.moveaxis(np.asarray(x, np.float32).astype(ml_dtypes.bfloat16).astype(np.float64), axis, -1)
    blocks = v.reshape(v.shape[:-1] + (-1, 32))
    amax = np.abs(blocks).max(-1, keepdims=True)
    byte = np.maximum(np.where(amax > 0, np.frexp(amax)[1] - 1 + 127, 0) - down, 1)
    scale = np.exp2(byte - 127.0)
    codes = (blocks / scale).astype(np.float32).astype(dtype).astype(np.float64)
    return np.moveaxis((codes * scale).reshape(v.shape), -1, axis)


WIDE = False


def mx_kscale(k):
    if not WIDE:
        return np.ones(k)
    levels = np.array([10, -10, 5, -5, 0])
    if k % 512:
        return np.exp2(np.random.permutation(np.resize(levels, k // 32))).repeat(32)
    a = np.empty((k // 512, 16))
    for p in range(k // 512):
        a[p, :8] = np.random.permutation(np.resize(levels, 8))
        for g in range(8):
            far = levels[np.abs(levels - a[p, g]) >= 10]
            a[p, g + 8] = far[np.random.randint(len(far))]
    return np.exp2(a.ravel()).repeat(32)


def f64(x):
    return np.asarray(x).astype(np.float64)


def striped(idx):
    return np.tile(np.asarray(idx).reshape(-1, 16).T, (8, 1)).astype(np.uint16)


def unstriped(offs):
    return offs[:16].T.reshape(-1).astype(np.int64)


E2M1 = np.array([0.0, 0.5, 1.0, 1.5, 2.0, 3.0, 4.0, 6.0, -0.0, -0.5, -1.0, -1.5, -2.0, -3.0, -4.0, -6.0])


def pack_weight(w, fmt):
    k, n = w.shape
    w = f64(np.asarray(w, np.float32).astype(ml_dtypes.bfloat16)).reshape(k // 32, 32, n)
    amax = np.abs(w).max(1)
    if fmt == "e4m3":
        byte = np.frexp(amax)[1] - 1 + 127 - 7
    else:
        mant, ex = np.frexp(amax / 6.0)
        byte = np.where(mant > 0.5, ex, ex - 1) + 127
    byte = np.clip(np.where(amax > 0, byte, 1), 1, 254)
    scaled = (w * np.exp2(127.0 - byte)[:, None, :]).reshape(k, n).astype(np.float32)
    by_word = np.ascontiguousarray(scaled.reshape(k // 512, 128, 4, n).transpose(0, 1, 3, 2))
    if fmt == "e4m3":
        words = by_word.astype(ml_dtypes.float8_e4m3fn).view(np.uint8)
    else:
        c = by_word.astype(ml_dtypes.float4_e2m1fn).view(np.uint8) & 0xF
        words = (c[..., 0::2] | (c[..., 1::2] << 4)).reshape(k // 512, 128, 2 * n)
    return np.ascontiguousarray(words), np.ascontiguousarray(byte.astype(np.uint8).reshape(k // 512, 16, n))


def unpack_weight(words, scales, fmt):
    g, _, n = scales.shape
    words = np.ascontiguousarray(words).reshape(g, 128, n, -1)
    if fmt == "e4m3":
        vals = words.view(ml_dtypes.float8_e4m3fn).astype(np.float64)
    else:
        nib = np.empty((g, 128, n, 4), np.uint8)
        nib[..., 0::2] = words & 0xF
        nib[..., 1::2] = words >> 4
        vals = E2M1[nib]
    vals = vals * np.repeat(np.exp2(scales.astype(np.float64) - 127.0), 8, axis=1)[..., None]
    return vals.transpose(0, 1, 3, 2).reshape(g * 512, n)


def e4m3fn_bytes(y):
    return np.clip(np.asarray(y, np.float64), -448.0, 448.0).astype(np.float32).astype(ml_dtypes.float8_e4m3fn).view(np.uint8)


def e4m3fn_values(b):
    return np.asarray(b, np.uint8).view(ml_dtypes.float8_e4m3fn).astype(np.float64)


K, T, J, R, V, O, N = 512, 1024, 256, 512, 512, 256, 256


def setup_inputs():
    n = np.random.standard_normal
    idx = np.random.permutation(T)[:J]
    idx2 = np.random.permutation(J)[:O]
    idx3 = np.random.permutation(V)[:O]
    fk = mx_kscale(K)
    fr = mx_kscale(R)
    xtp = pack_weight(n((K, T)) / fk[:, None], "e2m1")
    wp = pack_weight(n((K, R)) * 1 / np.sqrt(K) * fk[:, None] * fr, "e4m3")
    wbp = pack_weight(n((R, N)) * 1 / np.sqrt(R) / fr[:, None], "e2m1")
    return {
        "xt_words": xtp[0],
        "xt_scales": xtp[1],
        "w_words": wp[0],
        "w_scales": wp[1],
        "ca": e4m3fn_bytes(60.0 * n((R, V))),
        "ts": np.tile(np.random.uniform(0.004, 0.02, (1, V)), (128, 1)).astype(np.float32),
        "wb_words": wbp[0],
        "wb_scales": wbp[1],
        "offs": striped(idx),
        "offs2": striped(idx2),
        "offs3": striped(idx3),
    }


def reference(xt_words, xt_scales, w_words, w_scales, ca, ts, wb_words, wb_scales, offs, offs2, offs3):
    idx = unstriped(offs)
    idx2 = unstriped(offs2)
    idx3 = unstriped(offs3)
    xtu = unpack_weight(xt_words, xt_scales, "e2m1")
    wu = unpack_weight(w_words, w_scales, "e4m3")
    wbu = unpack_weight(wb_words, wb_scales, "e2m1")
    xtidxg = xtu[:, idx]
    a = wu.T @ xtidxg
    g1 = e4m3fn_values(ca)[:, idx3] * f64(ts)[:1][:, idx3]
    hid = a[:, idx2] * g1
    hidq = mxq(hid, 0, "e4m3")
    p = wbu.T @ hidq
    return p

@@ -1,0 +1,141 @@
+from contextlib import ExitStack
+
+import concourse.mybir as mybir
+
+K, T, J, R, V, O, N = 512, 1024, 256, 512, 512, 256, 256
+FLOPS = 2 * K * R * J + 2 * R * N * O
+
+F32 = mybir.dt.float32
+BF16 = mybir.dt.bfloat16
+I32 = mybir.dt.int32
+U32 = mybir.dt.uint32
+U16 = mybir.dt.uint16
+U8 = mybir.dt.uint8
+FP8 = mybir.dt.float8_e4m3fn
+FP8X4 = mybir.dt.float8_e4m3fn_x4
+FP4X4 = mybir.dt.float4_e2m1fn_x4
+MULT = mybir.AluOpType.mult
+COPY = mybir.ActivationFunctionType.Copy
+
+P = 128
+PACK = 4
+QUADS = 4
+HALF = O // 2
+
+
+def tile_list_ownsteps_kernel(
+    tc, xt_words, xt_scales, w_words, w_scales, ca, ts, wb_words, wb_scales, offs, offs2, offs3, out
+):
+    nc = tc.nc
+    with ExitStack() as ctx:
+        sb = ctx.enter_context(tc.tile_pool(name="sb", bufs=1))
+        ps = ctx.enter_context(tc.psum_pool(name="ps", bufs=1))
+
+        idx = sb.tile([P, J // 16], U16)
+        idx2 = sb.tile([P, O // 16], U16)
+        idx3 = sb.tile([P, O // 16], U16)
+        x_words = sb.tile([P, T], U16, align_bytes=64)
+        x_plane = sb.tile([P, T], U8, align_bytes=64)
+        w_raw = sb.tile([P, R], U32, align_bytes=64)
+        w_rows = sb.tile([4, QUADS, R // 4], I32, align_bytes=64)
+        w_plane = sb.tile([P, R], U8, align_bytes=64)
+        wb_sb = sb.tile([P, 2 * N], U8, align_bytes=64)
+        wb_plane = sb.tile([P, N], U8, align_bytes=64)
+        ts_sb = sb.tile([P, V], F32, align_bytes=64)
+        ca_sb = [sb.tile([P, V], U8, name=f"ca_sb{t}", align_bytes=64) for t in range(PACK)]
+
+        nc.vector.memset(w_plane[:].bitcast(I32), 0)
+        nc.vector.memset(wb_plane[:].bitcast(I32), 0)
+
+        nc.sync.dma_start(idx[:], offs)
+        nc.sync.dma_start(w_rows[:], w_scales[0].bitcast(I32).rearrange("(q r) c -> r q c", r=4))
+        for q in range(QUADS):
+            nc.sync.dma_start(
+                x_plane[32 * q : 32 * q + 32, :].bitcast(I32),
+                xt_scales[0, 4 * q : 4 * q + 4, :].bitcast(I32).partition_broadcast(8),
+            )
+        nc.sync.dma_start(w_raw[:].bitcast(I32), w_words[0].rearrange("p n t -> p (n t)").bitcast(I32))
+        nc.sync.dma_start(x_words[:].bitcast(I32), xt_words[0].bitcast(I32))
+        nc.sync.dma_start(idx3[:], offs3)
+        ca_rows = ca.rearrange("(p t) v -> p t v", t=PACK)
+        for t in range(PACK):
+            nc.sync.dma_start(ca_sb[t][:], ca_rows[:, t, :])
+            if t == 0:
+                nc.sync.dma_start(ts_sb[:], ts)
+        nc.sync.dma_start(idx2[:], offs2)
+        nc.sync.dma_start(wb_sb[:].bitcast(I32), wb_words[0].bitcast(I32))
+        for q in range(QUADS):
+            nc.sync.dma_start(wb_plane[32 * q : 32 * q + 4, :].bitcast(I32), wb_scales[0, 4 * q : 4 * q + 4, :].bitcast(I32))
+
+        for q in range(QUADS):
+            nc.vector.tensor_copy(w_plane[32 * q : 32 * q + 4, :].bitcast(I32), w_rows[:, q, :])
+        xg_plane = sb.tile([P, J], U8, align_bytes=64)
+        nc.vector.tensor_copy(xg_plane[:], x_plane[:].indirect(idx[:]))
+        w_dealt_plane = sb.tile([P, PACK, P], U8, align_bytes=64)
+        nc.vector.tensor_copy(w_dealt_plane[:], w_plane[:].rearrange("p (m t) -> p t m", t=PACK))
+        xg_words = sb.tile([P, J], U16, align_bytes=64)
+        nc.vector.tensor_copy(xg_words[:], x_words[:].indirect(idx[:]))
+        w_dealt = sb.tile([P, PACK, P], U32, align_bytes=64)
+        nc.scalar.copy(w_dealt[:].rearrange("p t m -> p m t"), w_raw[:].rearrange("p (m t) -> p m t", t=PACK))
+
+        ts_g = sb.tile([P, O], F32, align_bytes=64)
+        nc.scalar.activation(ts_g[:], ts_sb[:].indirect(idx3[:]), COPY)
+
+        a_sb = []
+        for t in range(PACK):
+            a_ps = ps.tile([P, J], F32, name=f"a_ps{t}")
+            nc.tensor.matmul_mx(
+                out=a_ps[:],
+                lhsT=w_dealt[:, t, :].bitcast(FP8X4),
+                lhsT_scale=w_dealt_plane[:, t, :],
+                rhs=xg_words[:].bitcast(FP4X4),
+                rhs_scale=xg_plane[:],
+                start=True,
+                stop=True,
+            )
+            a_t = sb.tile([P, J], F32, name=f"a_sb{t}", align_bytes=64)
+            nc.scalar.copy(a_t[:], a_ps[:])
+            a_sb.append(a_t)
+
+        ca_g = sb.tile([P, PACK, O], U8, align_bytes=64)
+        for t in range(PACK):
+            nc.vector.tensor_copy(ca_g[:, t, :], ca_sb[t][:].indirect(idx3[:]))
+        g1 = sb.tile([P, PACK, O], F32, align_bytes=64)
+        for t in range(PACK):
+            nc.vector.tensor_tensor(g1[:, t, :], ca_g[:, t, :].bitcast(FP8), ts_g[:], MULT)
+
+        a_g = [sb.tile([P, PACK, HALF], F32, name=f"a_g{h}", align_bytes=64) for h in range(2)]
+        for h in range(2):
+            for t in range(PACK):
+                nc.scalar.activation(a_g[h][:, t, :], a_sb[t][:].indirect(idx2[:, 8 * h : 8 * h + 8]), COPY)
+
+        hid = [sb.tile([P, HALF * PACK], BF16, name=f"hid{h}", align_bytes=64) for h in range(2)]
+        for h in range(2):
+            nc.vector.tensor_tensor(
+                hid[h][:].rearrange("p (c i t) -> p c t i", i=4, t=PACK),
+                a_g[h][:].rearrange("p t (c i) -> p c t i", i=4),
+                g1[:, :, h * HALF : (h + 1) * HALF].rearrange("p t (c i) -> p c t i", i=4),
+                MULT,
+            )
+        out_rows = out.rearrange("(b p) o -> p b o", p=P)
+        for h in range(2):
+            hid_words = sb.tile([P, HALF], U32, name=f"hid_words{h}", align_bytes=64)
+            hid_plane = sb.tile([P, HALF], U8, name=f"hid_plane{h}", align_bytes=64)
+            nc.vector.quantize_mx(out=hid_words[:].bitcast(FP8X4), scales=hid_plane[:], in_=hid[h][:])
+            res = sb.tile([P, 2, HALF], F32, name=f"res{h}", align_bytes=64)
+            for b in range(2):
+                o_ps = ps.tile([P, HALF], F32, name=f"o_ps{h}{b}")
+                nc.tensor.matmul_mx(
+                    out=o_ps[:],
+                    lhsT=wb_sb[:, 2 * P * b : 2 * P * (b + 1)].bitcast(FP4X4),
+                    lhsT_scale=wb_plane[:, P * b : P * (b + 1)],
+                    rhs=hid_words[:].bitcast(FP8X4),
+                    rhs_scale=hid_plane[:],
+                    start=True,
+                    stop=True,
+                )
+                if h == 1 and b == 1:
+                    nc.vector.tensor_copy(res[:, b, :], o_ps[:])
+                else:
+                    nc.scalar.copy(res[:, b, :], o_ps[:])
+            nc.sync.dma_start(out_rows[:, :, h * HALF : (h + 1) * HALF], res[:])

@@ -41,29 +41,31 @@ def tile_list_ownsteps_kernel(
         w_plane = sb.tile([P, R], U8, align_bytes=64)
         wb_sb = sb.tile([P, 2 * N], U8, align_bytes=64)
         wb_plane = sb.tile([P, N], U8, align_bytes=64)
-        ts_sb = sb.tile([P, V], F32, align_bytes=64)
+        ts_sb = sb.tile([P, V], F32, tag="window", align_bytes=64)
         ca_sb = [sb.tile([P, V], U8, name=f"ca_sb{t}", align_bytes=64) for t in range(PACK)]
 
         nc.vector.memset(w_plane[:].bitcast(I32), 0)
         nc.vector.memset(wb_plane[:].bitcast(I32), 0)
 
-        nc.sync.dma_start(idx[:], offs)
-        nc.sync.dma_start(w_rows[:], w_scales[0].bitcast(I32).rearrange("(q r) c -> r q c", r=4))
-        for q in range(QUADS):
-            nc.sync.dma_start(
+        def load_x_scales(queue, q):
+            queue.dma_start(
                 x_plane[32 * q : 32 * q + 32, :].bitcast(I32),
                 xt_scales[0, 4 * q : 4 * q + 4, :].bitcast(I32).partition_broadcast(8),
             )
-        nc.sync.dma_start(w_raw[:].bitcast(I32), w_words[0].rearrange("p n t -> p (n t)").bitcast(I32))
+
+        nc.sync.dma_start(idx[:], offs)
+        nc.scalar.dma_start(w_rows[:], w_scales[0].bitcast(I32).rearrange("(q r) c -> r q c", r=4))
+        for q in range(QUADS):
+            load_x_scales(nc.sync if q % 2 == 0 else nc.scalar, q)
         nc.sync.dma_start(x_words[:].bitcast(I32), xt_words[0].bitcast(I32))
+        nc.scalar.dma_start(w_raw[:].bitcast(I32), w_words[0].rearrange("p n t -> p (n t)").bitcast(I32))
+        nc.gpsimd.dma_start(ts_sb[:], ts)
+        nc.gpsimd.dma_start(wb_sb[:].bitcast(I32), wb_words[0].bitcast(I32))
         nc.sync.dma_start(idx3[:], offs3)
         ca_rows = ca.rearrange("(p t) v -> p t v", t=PACK)
         for t in range(PACK):
             nc.sync.dma_start(ca_sb[t][:], ca_rows[:, t, :])
-            if t == 0:
-                nc.sync.dma_start(ts_sb[:], ts)
         nc.sync.dma_start(idx2[:], offs2)
-        nc.sync.dma_start(wb_sb[:].bitcast(I32), wb_words[0].bitcast(I32))
         for q in range(QUADS):
             nc.sync.dma_start(wb_plane[32 * q : 32 * q + 4, :].bitcast(I32), wb_scales[0, 4 * q : 4 * q + 4, :].bitcast(I32))
 
@@ -76,12 +78,16 @@ def tile_list_ownsteps_kernel(
         xg_words = sb.tile([P, J], U16, align_bytes=64)
         nc.vector.tensor_copy(xg_words[:], x_words[:].indirect(idx[:]))
         w_dealt = sb.tile([P, PACK, P], U32, align_bytes=64)
-        nc.scalar.copy(w_dealt[:].rearrange("p t m -> p m t"), w_raw[:].rearrange("p (m t) -> p m t", t=PACK))
+        for u in range(2):
+            nc.scalar.copy(
+                w_dealt[:, 2 * u : 2 * u + 2, :].rearrange("p t m -> p m t"),
+                w_raw[:].rearrange("p (m t) -> p m t", t=PACK)[:, :, 2 * u : 2 * u + 2],
+            )
 
         ts_g = sb.tile([P, O], F32, align_bytes=64)
         nc.scalar.activation(ts_g[:], ts_sb[:].indirect(idx3[:]), COPY)
 
-        a_sb = []
+        a_sb = sb.tile([P, PACK * J], F32, tag="window", align_bytes=64)
         for t in range(PACK):
             a_ps = ps.tile([P, J], F32, name=f"a_ps{t}")
             nc.tensor.matmul_mx(
@@ -93,9 +99,7 @@ def tile_list_ownsteps_kernel(
                 start=True,
                 stop=True,
             )
-            a_t = sb.tile([P, J], F32, name=f"a_sb{t}", align_bytes=64)
-            nc.scalar.copy(a_t[:], a_ps[:])
-            a_sb.append(a_t)
+            nc.scalar.copy(a_sb[:, t * J : (t + 1) * J], a_ps[:])
 
         ca_g = sb.tile([P, PACK, O], U8, align_bytes=64)
         for t in range(PACK):
@@ -104,21 +108,25 @@ def tile_list_ownsteps_kernel(
         for t in range(PACK):
             nc.vector.tensor_tensor(g1[:, t, :], ca_g[:, t, :].bitcast(FP8), ts_g[:], MULT)
 
-        a_g = [sb.tile([P, PACK, HALF], F32, name=f"a_g{h}", align_bytes=64) for h in range(2)]
+        a_g = sb.tile([P, PACK, O], F32, align_bytes=64)
+        for t in range(PACK - 1):
+            nc.scalar.activation(a_g[:, t, :], a_sb[:, t * J : (t + 2) * J].indirect(idx2[:]), COPY)
         for h in range(2):
-            for t in range(PACK):
-                nc.scalar.activation(a_g[h][:, t, :], a_sb[t][:].indirect(idx2[:, 8 * h : 8 * h + 8]), COPY)
+            nc.scalar.activation(
+                a_g[:, PACK - 1, h * HALF : (h + 1) * HALF],
+                a_sb[:, (PACK - 1) * J :].indirect(idx2[:, 8 * h : 8 * h + 8]),
+                COPY,
+            )
 
+        out_rows = out.rearrange("(b p) o -> p b o", p=P)
         hid = [sb.tile([P, HALF * PACK], BF16, name=f"hid{h}", align_bytes=64) for h in range(2)]
         for h in range(2):
             nc.vector.tensor_tensor(
                 hid[h][:].rearrange("p (c i t) -> p c t i", i=4, t=PACK),
-                a_g[h][:].rearrange("p t (c i) -> p c t i", i=4),
+                a_g[:, :, h * HALF : (h + 1) * HALF].rearrange("p t (c i) -> p c t i", i=4),
                 g1[:, :, h * HALF : (h + 1) * HALF].rearrange("p t (c i) -> p c t i", i=4),
                 MULT,
             )
-        out_rows = out.rearrange("(b p) o -> p b o", p=P)
-        for h in range(2):
             hid_words = sb.tile([P, HALF], U32, name=f"hid_words{h}", align_bytes=64)
             hid_plane = sb.tile([P, HALF], U8, name=f"hid_plane{h}", align_bytes=64)
             nc.vector.quantize_mx(out=hid_words[:].bitcast(FP8X4), scales=hid_plane[:], in_=hid[h][:])
@@ -138,4 +146,8 @@ def tile_list_ownsteps_kernel(
                     nc.vector.tensor_copy(res[:, b, :], o_ps[:])
                 else:
                     nc.scalar.copy(res[:, b, :], o_ps[:])
-            nc.sync.dma_start(out_rows[:, :, h * HALF : (h + 1) * HALF], res[:])
+                if h == 1:
+                    queue = nc.scalar if b == 0 else nc.sync
+                    queue.dma_start(out_rows[:, b, HALF:O], res[:, b, :])
+            if h == 0:
+                nc.sync.dma_start(out_rows[:, :, 0:HALF], res[:])

@@ -88,6 +88,11 @@ def tile_list_ownsteps_kernel(
         nc.scalar.activation(ts_g[:], ts_sb[:].indirect(idx3[:]), COPY)
 
         a_sb = sb.tile([P, PACK * J], F32, tag="window", align_bytes=64)
+        a_g = sb.tile([P, PACK, O], F32, align_bytes=64)
+
+        def gather_plane(t):
+            nc.scalar.activation(a_g[:, t, :], a_sb[:, t * J : (t + 2) * J].indirect(idx2[:]), COPY)
+
         for t in range(PACK):
             a_ps = ps.tile([P, J], F32, name=f"a_ps{t}")
             nc.tensor.matmul_mx(
@@ -99,7 +104,11 @@ def tile_list_ownsteps_kernel(
                 start=True,
                 stop=True,
             )
+            if t == PACK - 1:
+                gather_plane(0)
             nc.scalar.copy(a_sb[:, t * J : (t + 1) * J], a_ps[:])
+        gather_plane(1)
+        gather_plane(2)
 
         ca_g = sb.tile([P, PACK, O], U8, align_bytes=64)
         for t in range(PACK):
@@ -108,15 +117,9 @@ def tile_list_ownsteps_kernel(
         for t in range(PACK):
             nc.vector.tensor_tensor(g1[:, t, :], ca_g[:, t, :].bitcast(FP8), ts_g[:], MULT)
 
-        a_g = sb.tile([P, PACK, O], F32, align_bytes=64)
-        for t in range(PACK - 1):
-            nc.scalar.activation(a_g[:, t, :], a_sb[:, t * J : (t + 2) * J].indirect(idx2[:]), COPY)
-        for h in range(2):
-            nc.scalar.activation(
-                a_g[:, PACK - 1, h * HALF : (h + 1) * HALF],
-                a_sb[:, (PACK - 1) * J :].indirect(idx2[:, 8 * h : 8 * h + 8]),
-                COPY,
-            )
+        last = PACK - 1
+        nc.vector.tensor_copy(a_g[:, last, :HALF], a_sb[:, last * J :].indirect(idx2[:, :8]))
+        nc.scalar.activation(a_g[:, last, HALF:], a_sb[:, last * J :].indirect(idx2[:, 8:]), COPY)
 
         out_rows = out.rearrange("(b p) o -> p b o", p=P)
         hid = [sb.tile([P, HALF * PACK], BF16, name=f"hid{h}", align_bytes=64) for h in range(2)]

from contextlib import ExitStack

import concourse.mybir as mybir

K, T, J, R, V, O, N = 512, 1024, 256, 512, 512, 256, 256
FLOPS = 2 * K * R * J + 2 * R * N * O

F32 = mybir.dt.float32
BF16 = mybir.dt.bfloat16
I32 = mybir.dt.int32
U32 = mybir.dt.uint32
U16 = mybir.dt.uint16
U8 = mybir.dt.uint8
FP8 = mybir.dt.float8_e4m3fn
FP8X4 = mybir.dt.float8_e4m3fn_x4
FP4X4 = mybir.dt.float4_e2m1fn_x4
MULT = mybir.AluOpType.mult
COPY = mybir.ActivationFunctionType.Copy

P = 128
PACK = 4
QUADS = 4
HALF = O // 2


def tile_list_ownsteps_kernel(
    tc, xt_words, xt_scales, w_words, w_scales, ca, ts, wb_words, wb_scales, offs, offs2, offs3, out
):
    nc = tc.nc
    with ExitStack() as ctx:
        sb = ctx.enter_context(tc.tile_pool(name="sb", bufs=1))
        ps = ctx.enter_context(tc.psum_pool(name="ps", bufs=1))

        idx = sb.tile([P, J // 16], U16)
        idx2 = sb.tile([P, O // 16], U16)
        idx3 = sb.tile([P, O // 16], U16)
        x_words = sb.tile([P, T], U16, align_bytes=64)
        x_plane = sb.tile([P, T], U8, align_bytes=64)
        w_raw = sb.tile([P, R], U32, align_bytes=64)
        w_rows = sb.tile([4, QUADS, R // 4], I32, align_bytes=64)
        w_plane = sb.tile([P, R], U8, align_bytes=64)
        wb_sb = sb.tile([P, 2 * N], U8, align_bytes=64)
        wb_plane = sb.tile([P, N], U8, align_bytes=64)
        ts_sb = sb.tile([P, V], F32, tag="window", align_bytes=64)
        ca_sb = [sb.tile([P, V], U8, name=f"ca_sb{t}", align_bytes=64) for t in range(PACK)]

        nc.vector.memset(w_plane[:].bitcast(I32), 0)
        nc.vector.memset(wb_plane[:].bitcast(I32), 0)

        def load_x_scales(queue, q):
            queue.dma_start(
                x_plane[32 * q : 32 * q + 32, :].bitcast(I32),
                xt_scales[0, 4 * q : 4 * q + 4, :].bitcast(I32).partition_broadcast(8),
            )

        nc.sync.dma_start(idx[:], offs)
        nc.scalar.dma_start(w_rows[:], w_scales[0].bitcast(I32).rearrange("(q r) c -> r q c", r=4))
        for q in range(QUADS):
            load_x_scales(nc.sync if q % 2 == 0 else nc.scalar, q)
        nc.sync.dma_start(x_words[:].bitcast(I32), xt_words[0].bitcast(I32))
        nc.scalar.dma_start(w_raw[:].bitcast(I32), w_words[0].rearrange("p n t -> p (n t)").bitcast(I32))
        nc.gpsimd.dma_start(ts_sb[:], ts)
        nc.gpsimd.dma_start(wb_sb[:].bitcast(I32), wb_words[0].bitcast(I32))
        nc.sync.dma_start(idx3[:], offs3)
        ca_rows = ca.rearrange("(p t) v -> p t v", t=PACK)
        for t in range(PACK):
            nc.sync.dma_start(ca_sb[t][:], ca_rows[:, t, :])
        nc.sync.dma_start(idx2[:], offs2)
        for q in range(QUADS):
            nc.sync.dma_start(wb_plane[32 * q : 32 * q + 4, :].bitcast(I32), wb_scales[0, 4 * q : 4 * q + 4, :].bitcast(I32))

        for q in range(QUADS):
            nc.vector.tensor_copy(w_plane[32 * q : 32 * q + 4, :].bitcast(I32), w_rows[:, q, :])
        xg_plane = sb.tile([P, J], U8, align_bytes=64)
        nc.vector.tensor_copy(xg_plane[:], x_plane[:].indirect(idx[:]))
        w_dealt_plane = sb.tile([P, PACK, P], U8, align_bytes=64)
        nc.vector.tensor_copy(w_dealt_plane[:], w_plane[:].rearrange("p (m t) -> p t m", t=PACK))
        xg_words = sb.tile([P, J], U16, align_bytes=64)
        nc.vector.tensor_copy(xg_words[:], x_words[:].indirect(idx[:]))
        w_dealt = sb.tile([P, PACK, P], U32, align_bytes=64)
        for u in range(2):
            nc.scalar.copy(
                w_dealt[:, 2 * u : 2 * u + 2, :].rearrange("p t m -> p m t"),
                w_raw[:].rearrange("p (m t) -> p m t", t=PACK)[:, :, 2 * u : 2 * u + 2],
            )

        ts_g = sb.tile([P, O], F32, align_bytes=64)
        nc.scalar.activation(ts_g[:], ts_sb[:].indirect(idx3[:]), COPY)

        a_sb = sb.tile([P, PACK * J], F32, tag="window", align_bytes=64)
        a_g = sb.tile([P, PACK, O], F32, align_bytes=64)

        def gather_plane(t):
            nc.scalar.activation(a_g[:, t, :], a_sb[:, t * J : (t + 2) * J].indirect(idx2[:]), COPY)

        for t in range(PACK):
            a_ps = ps.tile([P, J], F32, name=f"a_ps{t}")
            nc.tensor.matmul_mx(
                out=a_ps[:],
                lhsT=w_dealt[:, t, :].bitcast(FP8X4),
                lhsT_scale=w_dealt_plane[:, t, :],
                rhs=xg_words[:].bitcast(FP4X4),
                rhs_scale=xg_plane[:],
                start=True,
                stop=True,
            )
            if t == PACK - 1:
                gather_plane(0)
            nc.scalar.copy(a_sb[:, t * J : (t + 1) * J], a_ps[:])
        gather_plane(1)
        gather_plane(2)

        ca_g = sb.tile([P, PACK, O], U8, align_bytes=64)
        for t in range(PACK):
            nc.vector.tensor_copy(ca_g[:, t, :], ca_sb[t][:].indirect(idx3[:]))
        g1 = sb.tile([P, PACK, O], F32, align_bytes=64)
        for t in range(PACK):
            nc.vector.tensor_tensor(g1[:, t, :], ca_g[:, t, :].bitcast(FP8), ts_g[:], MULT)

        last = PACK - 1
        nc.vector.tensor_copy(a_g[:, last, :HALF], a_sb[:, last * J :].indirect(idx2[:, :8]))
        nc.scalar.activation(a_g[:, last, HALF:], a_sb[:, last * J :].indirect(idx2[:, 8:]), COPY)

        out_rows = out.rearrange("(b p) o -> p b o", p=P)
        hid = [sb.tile([P, HALF * PACK], BF16, name=f"hid{h}", align_bytes=64) for h in range(2)]
        for h in range(2):
            nc.vector.tensor_tensor(
                hid[h][:].rearrange("p (c i t) -> p c t i", i=4, t=PACK),
                a_g[:, :, h * HALF : (h + 1) * HALF].rearrange("p t (c i) -> p c t i", i=4),
                g1[:, :, h * HALF : (h + 1) * HALF].rearrange("p t (c i) -> p c t i", i=4),
                MULT,
            )
            hid_words = sb.tile([P, HALF], U32, name=f"hid_words{h}", align_bytes=64)
            hid_plane = sb.tile([P, HALF], U8, name=f"hid_plane{h}", align_bytes=64)
            nc.vector.quantize_mx(out=hid_words[:].bitcast(FP8X4), scales=hid_plane[:], in_=hid[h][:])
            res = sb.tile([P, 2, HALF], F32, name=f"res{h}", align_bytes=64)
            for b in range(2):
                o_ps = ps.tile([P, HALF], F32, name=f"o_ps{h}{b}")
                nc.tensor.matmul_mx(
                    out=o_ps[:],
                    lhsT=wb_sb[:, 2 * P * b : 2 * P * (b + 1)].bitcast(FP4X4),
                    lhsT_scale=wb_plane[:, P * b : P * (b + 1)],
                    rhs=hid_words[:].bitcast(FP8X4),
                    rhs_scale=hid_plane[:],
                    start=True,
                    stop=True,
                )
                if h == 1 and b == 1:
                    nc.vector.tensor_copy(res[:, b, :], o_ps[:])
                else:
                    nc.scalar.copy(res[:, b, :], o_ps[:])
                if h == 1:
                    queue = nc.scalar if b == 0 else nc.sync
                    queue.dma_start(out_rows[:, b, HALF:O], res[:, b, :])
            if h == 0:
                nc.sync.dma_start(out_rows[:, :, 0:HALF], res[:])
